import numpy as np
import ml_dtypes


def mxq(x, axis, fmt="e4m3"):
    dtype, down = {"e4m3": (ml_dtypes.float8_e4m3fn, 7), "e5m2": (ml_dtypes.float8_e5m2, 14)}[fmt]
    v = np.moveaxis(np.asarray(x, np.float32).astype(ml_dtypes.bfloat16).astype(np.float64), axis, -1)
    blocks = v.reshape(v.shape[:-1] + (-1, 32))
    amax = np.abs(blocks).max(-1, keepdims=True)
    byte = np.maximum(np.where(amax > 0, np.frexp(amax)[1] - 1 + 127, 0) - down, 1)
    scale = np.exp2(byte - 127.0)
    codes = (blocks / scale).astype(np.float32).astype(dtype).astype(np.float64)
    return np.moveaxis((codes * scale).reshape(v.shape), -1, axis)


WIDE = False


def mx_kscale(k):
    if not WIDE:
        return np.ones(k)
    levels = np.array([10, -10, 5, -5, 0])
    if k % 512:
        return np.exp2(np.random.permutation(np.resize(levels, k // 32))).repeat(32)
    a = np.empty((k // 512, 16))
    for p in range(k // 512):
        a[p, :8] = np.random.permutation(np.resize(levels, 8))
        for g in range(8):
            far = levels[np.abs(levels - a[p, g]) >= 10]
            a[p, g + 8] = far[np.random.randint(len(far))]
    return np.exp2(a.ravel()).repeat(32)


def f64(x):
    return np.asarray(x).astype(np.float64)


def striped(idx):
    return np.tile(idx.reshape(-1, 16).T, (8, 1)).astype(np.uint16)


def unstriped(offs):
    return offs[:16].T.reshape(-1).astype(np.int64)


def gelu(v):
    return 0.5 * v * (1.0 + np.tanh(np.sqrt(2.0 / np.pi) * (v + 0.044715 * v**3)))


K, T, E, C, N = 1536, 1536, 2, 256, 384


def by_expert(wq, xq):
    return np.concatenate([wq[e].T @ xq[:, e * C:(e + 1) * C] for e in range(E)], axis=1)


def setup_inputs():
    n = np.random.standard_normal
    s = mx_kscale(K)[:, None]
    return {
        "xT": (n((K, T)) * s).astype(np.float32),
        "w": (n((E, K, N)) / np.sqrt(K) / s[None]).astype(np.float32),
        "b": (0.3 * n((N, E))).astype(np.float32),
        "gate": np.tile(np.random.uniform(0.2, 1.0, E * C), (N, 1)).astype(np.float32),
        "offs": striped(np.random.permutation(T)[:E * C]),
    }


def reference(xT, w, b, gate, offs):
    idx = unstriped(offs)
    xq = mxq(f64(xT)[:, idx], 0, "e4m3")
    y = by_expert(mxq(f64(w), 1, "e4m3"), xq)
    y = gelu(y + np.repeat(f64(b), C, axis=1))
    out = np.zeros((N, T))
    out[:, idx] = f64(gate) * y
    return out

@@ -1,0 +1,195 @@
+from contextlib import ExitStack
+
+import concourse.mybir as mybir
+
+K, T, E, C, N = 1536, 1536, 2, 256, 384
+SLOTS = E * C
+P = 128
+PACK = 4
+PASSES = K // (P * PACK)
+BLOCKS = N // P
+
+FLOPS = 2 * K * N * SLOTS
+
+F32 = mybir.dt.float32
+BF16 = mybir.dt.bfloat16
+U32 = mybir.dt.uint32
+U16 = mybir.dt.uint16
+U8 = mybir.dt.uint8
+FP8X4 = mybir.dt.float8_e4m3fn_x4
+GELU = mybir.ActivationFunctionType.Gelu_apprx_tanh
+MULT = mybir.AluOpType.mult
+
+
+def interleave(copy, grouped, planes):
+    copy(
+        out=grouped.rearrange("p (c i) t -> p c t i", i=4),
+        in_=planes.rearrange("p t (c i) -> p c t i", i=4),
+    )
+
+
+def tile_routed_moe_kernel(tc, xT, w, b, gate, offs, out):
+    nc = tc.nc
+    with ExitStack() as ctx:
+        keep = ctx.enter_context(tc.tile_pool(name="keep", bufs=1))
+        psum = ctx.enter_context(tc.psum_pool(name="psum", bufs=1))
+
+        offsets = keep.tile([P, SLOTS // 16], U16, name="offsets")
+        bias = keep.tile([P, BLOCKS, E], F32, name="bias")
+        gates = keep.tile([P, SLOTS], F32, name="gates")
+        warm = keep.tile([P, 1], F32, name="warm")
+        warmed = keep.tile([P, 1], F32, name="warmed")
+
+        nc.sync.dma_start(offsets[:], offs)
+
+        x_planes = [[keep.tile([P, T], F32, name=f"x{a}{t}") for t in range(PACK)] for a in range(PASSES)]
+        picked = [keep.tile([P, PACK, SLOTS], F32, name=f"picked{a}") for a in range(PASSES)]
+        x_grouped = [[keep.tile([P, C, PACK], BF16, name=f"xg{a}{e}", align_bytes=64) for e in range(E)] for a in range(PASSES)]
+        x_codes = [[keep.tile([P, C], U32, name=f"xc{a}{e}", align_bytes=64) for e in range(E)] for a in range(PASSES)]
+        x_scales = [[keep.tile([P, C], U8, name=f"xs{a}{e}", align_bytes=64) for e in range(E)] for a in range(PASSES)]
+
+        pieces = {}
+
+        def weight_piece(e, a, n0, n1):
+            raw = keep.tile([P, PACK, n1 - n0], F32, name=f"wr{e}{a}{n0}")
+            grouped = keep.tile([P, n1 - n0, PACK], BF16, name=f"wg{e}{a}{n0}", align_bytes=64)
+            codes = keep.tile([P, n1 - n0], U32, name=f"wc{e}{a}{n0}", align_bytes=64)
+            scales = keep.tile([P, n1 - n0], U8, name=f"ws{e}{a}{n0}", align_bytes=64)
+            for n in range(n0, n1, P):
+                pieces[e, a, n // P] = (codes, scales, n - n0)
+            return raw, grouped, codes, scales, e, a, n0, n1
+
+        def load_w(piece):
+            raw, e, a, n0, n1 = piece[0], piece[4], piece[5], piece[6], piece[7]
+            rows = w[e, a * 512 : (a + 1) * 512, n0:n1]
+            nc.sync.dma_start(raw[:], rows.rearrange("(p t) n -> p t n", t=PACK))
+
+        def load_x(a, t):
+            rows = xT.rearrange("(a p t) n -> a p t n", p=P, t=PACK)
+            nc.sync.dma_start(x_planes[a][t][:], rows[a, :, t, :])
+
+        def group_w(copy, piece):
+            interleave(copy, piece[1][:], piece[0][:])
+
+        def quant_w(piece):
+            grouped, codes, scales, width = piece[1], piece[2], piece[3], piece[7] - piece[6]
+            cuts = [(0, 256), (256, 384)] if width == 384 else [(0, width)]
+            for lo, hi in cuts:
+                nc.vector.quantize_mx(
+                    out=codes[:, lo:hi].bitcast(FP8X4),
+                    scales=scales[:, lo:hi],
+                    in_=grouped[:, lo:hi, :].rearrange("p n t -> p (n t)"),
+                )
+
+        w0 = [weight_piece(0, a, 0, 384) for a in range(PASSES)]
+        w1 = [weight_piece(1, a, 0, 256) for a in range(PASSES)]
+        w1b = [weight_piece(1, a, 256, 384) for a in range(PASSES)]
+
+        for t in range(PACK):
+            load_x(0, t)
+        load_w(w0[0])
+        nc.sync.dma_start(bias[:], b.rearrange("(c p) e -> p c e", p=P))
+        for t in range(PACK):
+            load_x(1, t)
+        load_w(w0[1])
+        load_w(w0[2])
+        for t in range(PACK):
+            load_x(2, t)
+        nc.sync.dma_start(gates[:], gate[0:P, :])
+        for piece in w1:
+            load_w(piece)
+        for piece in w1b:
+            load_w(piece)
+
+        nc.vector.memset(warm[:], 0.0)
+        nc.scalar.activation(warmed[:], warm[:], GELU)
+        windows = [keep.tile([P, T], F32, name=f"window{c}") for c in range(BLOCKS)]
+        for c in range(BLOCKS):
+            nc.gpsimd.memset(windows[c][:], 0.0)
+
+        sums = [[psum.tile([P, C], F32, name=f"sum{c}{e}") for e in range(E)] for c in range(BLOCKS)]
+
+        def gather(a, t):
+            nc.vector.tensor_copy(picked[a][:, t, :], x_planes[a][t][:].indirect(offsets[:]))
+
+        def group_x(copy, a, e):
+            interleave(copy, x_grouped[a][e][:], picked[a][:, :, e * C : (e + 1) * C])
+
+        def quant_x(a, e):
+            nc.vector.quantize_mx(
+                out=x_codes[a][e][:].bitcast(FP8X4),
+                scales=x_scales[a][e][:],
+                in_=x_grouped[a][e][:].rearrange("p n t -> p (n t)"),
+            )
+
+        def multiply(c, e, a):
+            codes, scales, n = pieces[e, a, c]
+            nc.tensor.matmul_mx(
+                out=sums[c][e][:],
+                lhsT=codes[:, n : n + P].bitcast(FP8X4),
+                lhsT_scale=scales[:, n : n + P],
+                rhs=x_codes[a][e][:].bitcast(FP8X4),
+                rhs_scale=x_scales[a][e][:],
+                start=(a == 0),
+                stop=(a == PASSES - 1),
+            )
+
+        def finish(c, e):
+            y = keep.tile([P, C], F32, name=f"y{c}{e}")
+            z = keep.tile([P, C], F32, name=f"z{c}{e}")
+            nc.scalar.activation(y[:], sums[c][e][:], GELU, bias=bias[:, c, e : e + 1])
+            nc.gpsimd.tensor_tensor(z[:], y[:], gates[:, e * C : (e + 1) * C], MULT)
+            nc.vector.tensor_copy(windows[c][:].indirect(offsets[:, e * 16 : (e + 1) * 16]), z[:])
+
+        scopy, vcopy = nc.scalar.copy, nc.vector.tensor_copy
+
+        for t in range(PACK):
+            gather(0, t)
+        group_x(scopy, 0, 0)
+        group_x(scopy, 0, 1)
+        group_w(scopy, w0[0])
+        gather(1, 0)
+        gather(1, 1)
+        quant_x(0, 0)
+        quant_x(0, 1)
+        gather(1, 2)
+        quant_w(w0[0])
+        for c in range(BLOCKS):
+            multiply(c, 0, 0)
+        gather(1, 3)
+        group_x(scopy, 1, 0)
+        group_x(scopy, 1, 1)
+        group_w(scopy, w0[1])
+        group_w(scopy, w0[2])
+        gather(2, 0)
+        quant_x(1, 0)
+        quant_x(1, 1)
+        gather(2, 1)
+        quant_w(w0[1])
+        for c in range(BLOCKS):
+            multiply(c, 0, 1)
+        gather(2, 2)
+        quant_w(w0[2])
+        gather(2, 3)
+        group_x(vcopy, 2, 0)
+        group_x(scopy, 2, 1)
+        quant_x(2, 0)
+        for c in range(BLOCKS):
+            multiply(c, 0, 2)
+        for c in range(BLOCKS):
+            finish(c, 0)
+        quant_x(2, 1)
+        for a in range(PASSES):
+            group_w(scopy, w1[a])
+            quant_w(w1[a])
+            for c in range(2):
+                multiply(c, 1, a)
+        for c in range(2):
+            finish(c, 1)
+            nc.sync.dma_start(out[c * P : (c + 1) * P, :], windows[c][:])
+        for a in range(PASSES):
+            group_w(scopy, w1b[a])
+            quant_w(w1b[a])
+            multiply(2, 1, a)
+        finish(2, 1)
+        nc.sync.dma_start(out[2 * P : 3 * P, :], windows[2][:])

@@ -81,7 +81,8 @@ def tile_routed_moe_kernel(tc, xT, w, b, gate, offs, out):
                     in_=grouped[:, lo:hi, :].rearrange("p n t -> p (n t)"),
                 )
 
-        w0 = [weight_piece(0, a, 0, 384) for a in range(PASSES)]
+        w0 = [weight_piece(0, a, 0, 384) for a in range(2)]
+        w0c = weight_piece(0, 2, 0, 384)
         w1 = [weight_piece(1, a, 0, 256) for a in range(PASSES)]
         w1b = [weight_piece(1, a, 256, 384) for a in range(PASSES)]
 
@@ -92,9 +93,9 @@ def tile_routed_moe_kernel(tc, xT, w, b, gate, offs, out):
         for t in range(PACK):
             load_x(1, t)
         load_w(w0[1])
-        load_w(w0[2])
         for t in range(PACK):
             load_x(2, t)
+        load_w(w0c)
         nc.sync.dma_start(gates[:], gate[0:P, :])
         for piece in w1:
             load_w(piece)
@@ -122,6 +123,17 @@ def tile_routed_moe_kernel(tc, xT, w, b, gate, offs, out):
                 in_=x_grouped[a][e][:].rearrange("p n t -> p (n t)"),
             )
 
+        def group_part(copy, piece, lo, hi):
+            interleave(copy, piece[1][:, lo:hi, :], piece[0][:, :, lo:hi])
+
+        def quant_part(piece, lo, hi):
+            grouped, codes, scales = piece[1], piece[2], piece[3]
+            nc.vector.quantize_mx(
+                out=codes[:, lo:hi].bitcast(FP8X4),
+                scales=scales[:, lo:hi],
+                in_=grouped[:, lo:hi, :].rearrange("p n t -> p (n t)"),
+            )
+
         def multiply(c, e, a):
             codes, scales, n = pieces[e, a, c]
             nc.tensor.matmul_mx(
@@ -134,12 +146,18 @@ def tile_routed_moe_kernel(tc, xT, w, b, gate, offs, out):
                 stop=(a == PASSES - 1),
             )
 
-        def finish(c, e):
-            y = keep.tile([P, C], F32, name=f"y{c}{e}")
-            z = keep.tile([P, C], F32, name=f"z{c}{e}")
-            nc.scalar.activation(y[:], sums[c][e][:], GELU, bias=bias[:, c, e : e + 1])
-            nc.gpsimd.tensor_tensor(z[:], y[:], gates[:, e * C : (e + 1) * C], MULT)
-            nc.vector.tensor_copy(windows[c][:].indirect(offsets[:, e * 16 : (e + 1) * 16]), z[:])
+        ys = [[keep.tile([P, C], F32, name=f"y{c}{e}") for e in range(E)] for c in range(BLOCKS)]
+        zs = [[keep.tile([P, C], F32, name=f"z{c}{e}") for e in range(E)] for c in range(BLOCKS)]
+
+        def activate(c, e):
+            nc.scalar.activation(ys[c][e][:], sums[c][e][:], GELU, bias=bias[:, c, e : e + 1])
+            nc.gpsimd.tensor_tensor(zs[c][e][:], ys[c][e][:], gates[:, e * C : (e + 1) * C], MULT)
+
+        def scatter(c, e):
+            nc.vector.tensor_copy(windows[c][:].indirect(offsets[:, e * 16 : (e + 1) * 16]), zs[c][e][:])
+
+        def store(c):
+            nc.sync.dma_start(out[c * P : (c + 1) * P, :], windows[c][:])
 
         scopy, vcopy = nc.scalar.copy, nc.vector.tensor_copy
 
@@ -160,36 +178,56 @@ def tile_routed_moe_kernel(tc, xT, w, b, gate, offs, out):
         group_x(scopy, 1, 0)
         group_x(scopy, 1, 1)
         group_w(scopy, w0[1])
-        group_w(scopy, w0[2])
         gather(2, 0)
+        gather(2, 1)
         quant_x(1, 0)
         quant_x(1, 1)
-        gather(2, 1)
+        gather(2, 2)
         quant_w(w0[1])
         for c in range(BLOCKS):
             multiply(c, 0, 1)
-        gather(2, 2)
-        quant_w(w0[2])
         gather(2, 3)
         group_x(vcopy, 2, 0)
         group_x(scopy, 2, 1)
         quant_x(2, 0)
-        for c in range(BLOCKS):
-            multiply(c, 0, 2)
-        for c in range(BLOCKS):
-            finish(c, 0)
+        group_part(vcopy, w0c, 0, 256)
+        group_part(scopy, w0c, 256, 384)
+        quant_part(w0c, 0, 256)
+        multiply(0, 0, 2)
+        multiply(1, 0, 2)
+        activate(0, 0)
+        activate(1, 0)
         quant_x(2, 1)
-        for a in range(PASSES):
-            group_w(scopy, w1[a])
-            quant_w(w1[a])
-            for c in range(2):
-                multiply(c, 1, a)
+        quant_part(w0c, 256, 384)
+        multiply(2, 0, 2)
+        activate(2, 0)
+        group_w(vcopy, w1[0])
+        group_w(scopy, w1[1])
+        quant_w(w1[0])
         for c in range(2):
-            finish(c, 1)
-            nc.sync.dma_start(out[c * P : (c + 1) * P, :], windows[c][:])
+            multiply(c, 1, 0)
+        scatter(0, 0)
+        group_w(scopy, w1[2])
+        quant_w(w1[1])
+        for c in range(2):
+            multiply(c, 1, 1)
+        scatter(1, 0)
+        quant_w(w1[2])
+        for c in range(2):
+            multiply(c, 1, 2)
+        group_w(scopy, w1b[0])
+        activate(0, 1)
+        activate(1, 1)
+        scatter(2, 0)
+        group_w(scopy, w1b[1])
+        group_w(vcopy, w1b[2])
+        scatter(0, 1)
+        store(0)
         for a in range(PASSES):
-            group_w(scopy, w1b[a])
             quant_w(w1b[a])
             multiply(2, 1, a)
-        finish(2, 1)
-        nc.sync.dma_start(out[2 * P : 3 * P, :], windows[2][:])
+        activate(2, 1)
+        scatter(1, 1)
+        store(1)
+        scatter(2, 1)
+        store(2)

@@ -30,6 +30,7 @@ def interleave(copy, grouped, planes):
 
 def tile_routed_moe_kernel(tc, xT, w, b, gate, offs, out):
     nc = tc.nc
+    scopy, vcopy = nc.scalar.copy, nc.vector.tensor_copy
     with ExitStack() as ctx:
         keep = ctx.enter_context(tc.tile_pool(name="keep", bufs=1))
         psum = ctx.enter_context(tc.psum_pool(name="psum", bufs=1))
@@ -39,195 +40,170 @@ def tile_routed_moe_kernel(tc, xT, w, b, gate, offs, out):
         gates = keep.tile([P, SLOTS], F32, name="gates")
         warm = keep.tile([P, 1], F32, name="warm")
         warmed = keep.tile([P, 1], F32, name="warmed")
-
-        nc.sync.dma_start(offsets[:], offs)
-
         x_planes = [[keep.tile([P, T], F32, name=f"x{a}{t}") for t in range(PACK)] for a in range(PASSES)]
         picked = [keep.tile([P, PACK, SLOTS], F32, name=f"picked{a}") for a in range(PASSES)]
-        x_grouped = [[keep.tile([P, C, PACK], BF16, name=f"xg{a}{e}", align_bytes=64) for e in range(E)] for a in range(PASSES)]
-        x_codes = [[keep.tile([P, C], U32, name=f"xc{a}{e}", align_bytes=64) for e in range(E)] for a in range(PASSES)]
-        x_scales = [[keep.tile([P, C], U8, name=f"xs{a}{e}", align_bytes=64) for e in range(E)] for a in range(PASSES)]
-
-        pieces = {}
-
-        def weight_piece(e, a, n0, n1):
-            raw = keep.tile([P, PACK, n1 - n0], F32, name=f"wr{e}{a}{n0}")
-            grouped = keep.tile([P, n1 - n0, PACK], BF16, name=f"wg{e}{a}{n0}", align_bytes=64)
-            codes = keep.tile([P, n1 - n0], U32, name=f"wc{e}{a}{n0}", align_bytes=64)
-            scales = keep.tile([P, n1 - n0], U8, name=f"ws{e}{a}{n0}", align_bytes=64)
-            for n in range(n0, n1, P):
-                pieces[e, a, n // P] = (codes, scales, n - n0)
-            return raw, grouped, codes, scales, e, a, n0, n1
-
-        def load_w(piece):
-            raw, e, a, n0, n1 = piece[0], piece[4], piece[5], piece[6], piece[7]
-            rows = w[e, a * 512 : (a + 1) * 512, n0:n1]
-            nc.sync.dma_start(raw[:], rows.rearrange("(p t) n -> p t n", t=PACK))
+        x_grouped = [keep.tile([P, SLOTS, PACK], BF16, name=f"xg{a}", align_bytes=64) for a in range(PASSES)]
+        x_codes = [keep.tile([P, SLOTS], U32, name=f"xc{a}", align_bytes=64) for a in range(PASSES)]
+        x_scales = [keep.tile([P, SLOTS], U8, name=f"xs{a}", align_bytes=64) for a in range(PASSES)]
+        w_raw = [[keep.tile([P, PACK, N], F32, name=f"wr{e}{a}") for a in range(PASSES)] for e in range(E)]
+        w_grouped = [[keep.tile([P, N, PACK], BF16, name=f"wg{e}{a}", align_bytes=64) for a in range(PASSES)] for e in range(E)]
+        w_codes = [[keep.tile([P, N], U32, name=f"wc{e}{a}", align_bytes=64) for a in range(PASSES)] for e in range(E)]
+        w_scales = [[keep.tile([P, N], U8, name=f"ws{e}{a}", align_bytes=64) for a in range(PASSES)] for e in range(E)]
+        windows = [keep.tile([P, T], F32, name=f"window{c}") for c in range(BLOCKS)]
+        ys = [[keep.tile([P, C], F32, name=f"y{c}{e}") for e in range(E)] for c in range(BLOCKS)]
+        sums = [[psum.tile([P, C], F32, name=f"sum{c}{e}") for e in range(E)] for c in range(BLOCKS)]
 
         def load_x(a, t):
             rows = xT.rearrange("(a p t) n -> a p t n", p=P, t=PACK)
             nc.sync.dma_start(x_planes[a][t][:], rows[a, :, t, :])
 
-        def group_w(copy, piece):
-            interleave(copy, piece[1][:], piece[0][:])
+        def load_w(e, a, n0=0, n1=N):
+            rows = w[e, a * 512 : (a + 1) * 512, n0:n1]
+            nc.sync.dma_start(w_raw[e][a][:, :, n0:n1], rows.rearrange("(p t) n -> p t n", t=PACK))
 
-        def quant_w(piece):
-            grouped, codes, scales, width = piece[1], piece[2], piece[3], piece[7] - piece[6]
-            cuts = [(0, 256), (256, 384)] if width == 384 else [(0, width)]
-            for lo, hi in cuts:
-                nc.vector.quantize_mx(
-                    out=codes[:, lo:hi].bitcast(FP8X4),
-                    scales=scales[:, lo:hi],
-                    in_=grouped[:, lo:hi, :].rearrange("p n t -> p (n t)"),
-                )
+        def gather(a, t, lo=0, hi=SLOTS):
+            nc.vector.tensor_copy(picked[a][:, t, lo:hi], x_planes[a][t][:].indirect(offsets[:, lo // 16 : hi // 16]))
 
-        w0 = [weight_piece(0, a, 0, 384) for a in range(2)]
-        w0c = weight_piece(0, 2, 0, 384)
-        w1 = [weight_piece(1, a, 0, 256) for a in range(PASSES)]
-        w1b = [weight_piece(1, a, 256, 384) for a in range(PASSES)]
+        def group_x(copy, a, lo, hi):
+            interleave(copy, x_grouped[a][:, lo:hi, :], picked[a][:, :, lo:hi])
 
-        for t in range(PACK):
-            load_x(0, t)
-        load_w(w0[0])
-        nc.sync.dma_start(bias[:], b.rearrange("(c p) e -> p c e", p=P))
-        for t in range(PACK):
-            load_x(1, t)
-        load_w(w0[1])
-        for t in range(PACK):
-            load_x(2, t)
-        load_w(w0c)
-        nc.sync.dma_start(gates[:], gate[0:P, :])
-        for piece in w1:
-            load_w(piece)
-        for piece in w1b:
-            load_w(piece)
-
-        nc.vector.memset(warm[:], 0.0)
-        nc.scalar.activation(warmed[:], warm[:], GELU)
-        windows = [keep.tile([P, T], F32, name=f"window{c}") for c in range(BLOCKS)]
-        for c in range(BLOCKS):
-            nc.gpsimd.memset(windows[c][:], 0.0)
-
-        sums = [[psum.tile([P, C], F32, name=f"sum{c}{e}") for e in range(E)] for c in range(BLOCKS)]
-
-        def gather(a, t):
-            nc.vector.tensor_copy(picked[a][:, t, :], x_planes[a][t][:].indirect(offsets[:]))
-
-        def group_x(copy, a, e):
-            interleave(copy, x_grouped[a][e][:], picked[a][:, :, e * C : (e + 1) * C])
-
-        def quant_x(a, e):
+        def quant_x(a, lo, hi):
             nc.vector.quantize_mx(
-                out=x_codes[a][e][:].bitcast(FP8X4),
-                scales=x_scales[a][e][:],
-                in_=x_grouped[a][e][:].rearrange("p n t -> p (n t)"),
+                out=x_codes[a][:, lo:hi].bitcast(FP8X4),
+                scales=x_scales[a][:, lo:hi],
+                in_=x_grouped[a][:, lo:hi, :].rearrange("p n t -> p (n t)"),
             )
 
-        def group_part(copy, piece, lo, hi):
-            interleave(copy, piece[1][:, lo:hi, :], piece[0][:, :, lo:hi])
+        def group_w(copy, e, a, lo, hi):
+            interleave(copy, w_grouped[e][a][:, lo:hi, :], w_raw[e][a][:, :, lo:hi])
 
-        def quant_part(piece, lo, hi):
-            grouped, codes, scales = piece[1], piece[2], piece[3]
+        def quant_w(e, a, lo, hi):
             nc.vector.quantize_mx(
-                out=codes[:, lo:hi].bitcast(FP8X4),
-                scales=scales[:, lo:hi],
-                in_=grouped[:, lo:hi, :].rearrange("p n t -> p (n t)"),
+                out=w_codes[e][a][:, lo:hi].bitcast(FP8X4),
+                scales=w_scales[e][a][:, lo:hi],
+                in_=w_grouped[e][a][:, lo:hi, :].rearrange("p n t -> p (n t)"),
             )
 
         def multiply(c, e, a):
-            codes, scales, n = pieces[e, a, c]
+            features = slice(c * P, (c + 1) * P)
+            slots = slice(e * C, (e + 1) * C)
             nc.tensor.matmul_mx(
                 out=sums[c][e][:],
-                lhsT=codes[:, n : n + P].bitcast(FP8X4),
-                lhsT_scale=scales[:, n : n + P],
-                rhs=x_codes[a][e][:].bitcast(FP8X4),
-                rhs_scale=x_scales[a][e][:],
+                lhsT=w_codes[e][a][:, features].bitcast(FP8X4),
+                lhsT_scale=w_scales[e][a][:, features],
+                rhs=x_codes[a][:, slots].bitcast(FP8X4),
+                rhs_scale=x_scales[a][:, slots],
                 start=(a == 0),
                 stop=(a == PASSES - 1),
             )
 
-        ys = [[keep.tile([P, C], F32, name=f"y{c}{e}") for e in range(E)] for c in range(BLOCKS)]
-        zs = [[keep.tile([P, C], F32, name=f"z{c}{e}") for e in range(E)] for c in range(BLOCKS)]
-
         def activate(c, e):
             nc.scalar.activation(ys[c][e][:], sums[c][e][:], GELU, bias=bias[:, c, e : e + 1])
-            nc.gpsimd.tensor_tensor(zs[c][e][:], ys[c][e][:], gates[:, e * C : (e + 1) * C], MULT)
 
         def scatter(c, e):
-            nc.vector.tensor_copy(windows[c][:].indirect(offsets[:, e * 16 : (e + 1) * 16]), zs[c][e][:])
+            nc.vector.tensor_tensor(
+                windows[c][:].indirect(offsets[:, e * 16 : (e + 1) * 16]), ys[c][e][:], gates[:, e * C : (e + 1) * C], MULT
+            )
 
         def store(c):
             nc.sync.dma_start(out[c * P : (c + 1) * P, :], windows[c][:])
 
-        scopy, vcopy = nc.scalar.copy, nc.vector.tensor_copy
-
+        nc.sync.dma_start(offsets[:], offs)
+        load_x(0, 0)
+        load_x(0, 1)
+        load_x(0, 2)
+        load_x(0, 3)
+        load_x(1, 0)
+        load_x(1, 1)
+        load_x(1, 2)
+        load_x(1, 3)
+        load_x(2, 0)
+        load_x(2, 1)
+        load_x(2, 2)
+        load_x(2, 3)
+        load_w(0, 0)
+        load_w(0, 1)
+        load_w(0, 2)
+        nc.sync.dma_start(bias[:], b.rearrange("(c p) e -> p c e", p=P))
+        load_w(1, 0)
+        nc.sync.dma_start(gates[:], gate[0:P, :])
+        load_w(1, 1)
+        load_w(1, 2)
+        nc.vector.memset(warm[:], 0.0)
+        nc.scalar.activation(warmed[:], warm[:], GELU)
+        for c in range(BLOCKS):
+            nc.gpsimd.memset(windows[c][:], 0.0)
         for t in range(PACK):
             gather(0, t)
-        group_x(scopy, 0, 0)
-        group_x(scopy, 0, 1)
-        group_w(scopy, w0[0])
+        group_x(scopy, 0, 0, 512)
         gather(1, 0)
         gather(1, 1)
-        quant_x(0, 0)
-        quant_x(0, 1)
+        quant_x(0, 0, 512)
         gather(1, 2)
-        quant_w(w0[0])
-        for c in range(BLOCKS):
-            multiply(c, 0, 0)
         gather(1, 3)
-        group_x(scopy, 1, 0)
-        group_x(scopy, 1, 1)
-        group_w(scopy, w0[1])
+        group_x(scopy, 1, 0, 512)
         gather(2, 0)
         gather(2, 1)
-        quant_x(1, 0)
-        quant_x(1, 1)
+        quant_x(1, 0, 512)
         gather(2, 2)
-        quant_w(w0[1])
-        for c in range(BLOCKS):
+        gather(2, 3, 0, C)
+        group_x(vcopy, 2, 0, 128)
+        group_x(scopy, 2, 128, 256)
+        gather(2, 3, C, SLOTS)
+        group_w(scopy, 0, 0, 0, 256)
+        quant_x(2, 0, 256)
+        group_x(vcopy, 2, 256, 448)
+        group_w(scopy, 0, 0, 256, 384)
+        quant_w(0, 0, 0, 256)
+        group_w(vcopy, 0, 1, 0, 128)
+        group_w(scopy, 0, 1, 128, 256)
+        quant_w(0, 0, 256, 384)
+        group_w(scopy, 0, 1, 256, 384)
+        quant_w(0, 1, 0, 256)
+        group_w(vcopy, 0, 2, 0, 256)
+        for c in (0, 1):
+            multiply(c, 0, 0)
             multiply(c, 0, 1)
-        gather(2, 3)
-        group_x(vcopy, 2, 0)
-        group_x(scopy, 2, 1)
-        quant_x(2, 0)
-        group_part(vcopy, w0c, 0, 256)
-        group_part(scopy, w0c, 256, 384)
-        quant_part(w0c, 0, 256)
+        group_w(scopy, 0, 2, 256, 384)
+        quant_w(0, 2, 0, 256)
+        group_x(scopy, 2, 448, 512)
+        quant_w(0, 2, 256, 384)
         multiply(0, 0, 2)
         multiply(1, 0, 2)
         activate(0, 0)
-        activate(1, 0)
-        quant_x(2, 1)
-        quant_part(w0c, 256, 384)
-        multiply(2, 0, 2)
-        activate(2, 0)
-        group_w(vcopy, w1[0])
-        group_w(scopy, w1[1])
-        quant_w(w1[0])
-        for c in range(2):
-            multiply(c, 1, 0)
+        quant_x(2, 256, 512)
+        group_w(scopy, 1, 0, 192, 384)
+        quant_w(0, 1, 256, 384)
         scatter(0, 0)
-        group_w(scopy, w1[2])
-        quant_w(w1[1])
-        for c in range(2):
-            multiply(c, 1, 1)
-        scatter(1, 0)
-        quant_w(w1[2])
-        for c in range(2):
-            multiply(c, 1, 2)
-        group_w(scopy, w1b[0])
-        activate(0, 1)
-        activate(1, 1)
-        scatter(2, 0)
-        group_w(scopy, w1b[1])
-        group_w(vcopy, w1b[2])
-        scatter(0, 1)
-        store(0)
         for a in range(PASSES):
-            quant_w(w1b[a])
-            multiply(2, 1, a)
+            multiply(2, 0, a)
+        group_w(scopy, 1, 0, 0, 192)
+        activate(1, 0)
+        quant_w(1, 0, 0, 256)
+        group_w(scopy, 1, 1, 192, 384)
+        quant_w(1, 0, 256, 384)
+        multiply(0, 1, 0)
+        multiply(1, 1, 0)
+        multiply(2, 1, 0)
+        scatter(1, 0)
+        activate(2, 0)
+        group_w(scopy, 1, 2, 256, 384)
+        group_w(scopy, 1, 2, 0, 256)
+        quant_w(1, 2, 256, 384)
+        quant_w(1, 1, 256, 384)
+        scatter(2, 0)
+        group_w(scopy, 1, 1, 0, 192)
+        multiply(2, 1, 1)
+        multiply(2, 1, 2)
         activate(2, 1)
-        scatter(1, 1)
-        store(1)
+        quant_w(1, 2, 0, 256)
+        quant_w(1, 1, 0, 256)
         scatter(2, 1)
         store(2)
+        for c in (1, 0):
+            multiply(c, 1, 1)
+            multiply(c, 1, 2)
+            activate(c, 1)
+        for c in (1, 0):
+            scatter(c, 1)
+            store(c)

@@ -1,13 +1,21 @@
 from contextlib import ExitStack
 
 import concourse.mybir as mybir
+from concourse.masks import make_identity
 
 K, T, E, C, N = 1536, 1536, 2, 256, 384
 SLOTS = E * C
 P = 128
 PACK = 4
-PASSES = K // (P * PACK)
-BLOCKS = N // P
+K_PASS = P * PACK
+PASSES = K // K_PASS
+FEATURE_TILES = N // P
+LIST_ROWS = 16
+LAST_PASS, LAST_T = PASSES - 1, PACK - 1
+
+TWO_TILES, ONE_TILE = (0, 2 * P), (2 * P, N)
+X_CUT = (128, C + 192)
+W1_CUT = 192
 
 FLOPS = 2 * K * N * SLOTS
 
@@ -23,66 +31,78 @@ MULT = mybir.AluOpType.mult
 
 def interleave(copy, grouped, planes):
     copy(
-        out=grouped.rearrange("p (c i) t -> p c t i", i=4),
-        in_=planes.rearrange("p t (c i) -> p c t i", i=4),
+        out=grouped.rearrange("p (n i) t -> p n t i", i=4),
+        in_=planes.rearrange("p t (n i) -> p n t i", i=4),
+    )
+
+
+def quantize(nc, codes, scales, grouped):
+    nc.vector.quantize_mx(
+        out=codes.bitcast(FP8X4),
+        scales=scales,
+        in_=grouped.rearrange("p n t -> p (n t)"),
     )
 
 
 def tile_routed_moe_kernel(tc, xT, w, b, gate, offs, out):
     nc = tc.nc
-    scopy, vcopy = nc.scalar.copy, nc.vector.tensor_copy
+    by_scalar, by_vector = nc.scalar.copy, nc.vector.tensor_copy
+
     with ExitStack() as ctx:
         keep = ctx.enter_context(tc.tile_pool(name="keep", bufs=1))
         psum = ctx.enter_context(tc.psum_pool(name="psum", bufs=1))
 
-        offsets = keep.tile([P, SLOTS // 16], U16, name="offsets")
-        bias = keep.tile([P, BLOCKS, E], F32, name="bias")
+        offsets = keep.tile([P, SLOTS // LIST_ROWS], U16, name="offsets")
         gates = keep.tile([P, SLOTS], F32, name="gates")
-        warm = keep.tile([P, 1], F32, name="warm")
-        warmed = keep.tile([P, 1], F32, name="warmed")
-        x_planes = [[keep.tile([P, T], F32, name=f"x{a}{t}") for t in range(PACK)] for a in range(PASSES)]
+        bias = keep.tile([P, E, FEATURE_TILES], F32, name="bias")
+        bias_rows = keep.tile([P, E * P], F32, name="bias_rows")
+        identity = keep.tile([P, P], F32, name="identity")
+        table_in = keep.tile([P, 1], F32, name="table_in")
+        table_out = keep.tile([P, 1], F32, name="table_out")
+
+        x_planes = [[keep.tile([P, T], F32, name=f"x_plane{a}{t}") for t in range(PACK)] for a in range(PASSES)]
         picked = [keep.tile([P, PACK, SLOTS], F32, name=f"picked{a}") for a in range(PASSES)]
-        x_grouped = [keep.tile([P, SLOTS, PACK], BF16, name=f"xg{a}", align_bytes=64) for a in range(PASSES)]
-        x_codes = [keep.tile([P, SLOTS], U32, name=f"xc{a}", align_bytes=64) for a in range(PASSES)]
-        x_scales = [keep.tile([P, SLOTS], U8, name=f"xs{a}", align_bytes=64) for a in range(PASSES)]
-        w_raw = [[keep.tile([P, PACK, N], F32, name=f"wr{e}{a}") for a in range(PASSES)] for e in range(E)]
-        w_grouped = [[keep.tile([P, N, PACK], BF16, name=f"wg{e}{a}", align_bytes=64) for a in range(PASSES)] for e in range(E)]
-        w_codes = [[keep.tile([P, N], U32, name=f"wc{e}{a}", align_bytes=64) for a in range(PASSES)] for e in range(E)]
-        w_scales = [[keep.tile([P, N], U8, name=f"ws{e}{a}", align_bytes=64) for a in range(PASSES)] for e in range(E)]
-        windows = [keep.tile([P, T], F32, name=f"window{c}") for c in range(BLOCKS)]
-        ys = [[keep.tile([P, C], F32, name=f"y{c}{e}") for e in range(E)] for c in range(BLOCKS)]
-        sums = [[psum.tile([P, C], F32, name=f"sum{c}{e}") for e in range(E)] for c in range(BLOCKS)]
+        x_grouped = [keep.tile([P, SLOTS, PACK], BF16, name=f"x_grouped{a}", align_bytes=64) for a in range(PASSES)]
+        x_codes = [keep.tile([P, SLOTS], U32, name=f"x_codes{a}", align_bytes=64) for a in range(PASSES)]
+        x_scales = [keep.tile([P, SLOTS], U8, name=f"x_scales{a}", align_bytes=64) for a in range(PASSES)]
+
+        def weight_tiles(name, shape, dtype):
+            return [[keep.tile(shape, dtype, name=f"{name}{e}{a}", align_bytes=64) for a in range(PASSES)] for e in range(E)]
+
+        w_raw = weight_tiles("w_raw", [P, PACK, N], F32)
+        w_grouped = weight_tiles("w_grouped", [P, N, PACK], BF16)
+        w_codes = weight_tiles("w_codes", [P, N], U32)
+        w_scales = weight_tiles("w_scales", [P, N], U8)
+
+        windows = [keep.tile([P, T], F32, name=f"window{c}") for c in range(FEATURE_TILES)]
+        activated = [[keep.tile([P, C], F32, name=f"activated{c}{e}") for e in range(E)] for c in range(FEATURE_TILES)]
+        sums = [[psum.tile([P, C], F32, name=f"sums{c}{e}") for e in range(E)] for c in range(FEATURE_TILES)]
+        bias_columns = psum.tile([P, E, P], F32, name="bias_columns")
 
         def load_x(a, t):
             rows = xT.rearrange("(a p t) n -> a p t n", p=P, t=PACK)
             nc.sync.dma_start(x_planes[a][t][:], rows[a, :, t, :])
 
-        def load_w(e, a, n0=0, n1=N):
-            rows = w[e, a * 512 : (a + 1) * 512, n0:n1]
-            nc.sync.dma_start(w_raw[e][a][:, :, n0:n1], rows.rearrange("(p t) n -> p t n", t=PACK))
+        def load_w(e, a):
+            rows = w[e, a * K_PASS : (a + 1) * K_PASS, :]
+            nc.sync.dma_start(w_raw[e][a][:], rows.rearrange("(p t) n -> p t n", t=PACK))
 
-        def gather(a, t, lo=0, hi=SLOTS):
-            nc.vector.tensor_copy(picked[a][:, t, lo:hi], x_planes[a][t][:].indirect(offsets[:, lo // 16 : hi // 16]))
+        def gather(a, t, start=0, stop=SLOTS):
+            columns = slice(start // LIST_ROWS, stop // LIST_ROWS)
+            nc.vector.tensor_copy(picked[a][:, t, start:stop], x_planes[a][t][:].indirect(offsets[:, columns]))
 
-        def group_x(copy, a, lo, hi):
-            interleave(copy, x_grouped[a][:, lo:hi, :], picked[a][:, :, lo:hi])
+        def group_x(copy, a, start, stop):
+            interleave(copy, x_grouped[a][:, start:stop, :], picked[a][:, :, start:stop])
 
-        def quant_x(a, lo, hi):
-            nc.vector.quantize_mx(
-                out=x_codes[a][:, lo:hi].bitcast(FP8X4),
-                scales=x_scales[a][:, lo:hi],
-                in_=x_grouped[a][:, lo:hi, :].rearrange("p n t -> p (n t)"),
-            )
+        def quantize_x(a, start, stop):
+            quantize(nc, x_codes[a][:, start:stop], x_scales[a][:, start:stop], x_grouped[a][:, start:stop, :])
 
-        def group_w(copy, e, a, lo, hi):
-            interleave(copy, w_grouped[e][a][:, lo:hi, :], w_raw[e][a][:, :, lo:hi])
+        def group_w(copy, e, a, start, stop):
+            interleave(copy, w_grouped[e][a][:, start:stop, :], w_raw[e][a][:, :, start:stop])
 
-        def quant_w(e, a, lo, hi):
-            nc.vector.quantize_mx(
-                out=w_codes[e][a][:, lo:hi].bitcast(FP8X4),
-                scales=w_scales[e][a][:, lo:hi],
-                in_=w_grouped[e][a][:, lo:hi, :].rearrange("p n t -> p (n t)"),
-            )
+        def quantize_w(e, a, features):
+            start, stop = features
+            quantize(nc, w_codes[e][a][:, start:stop], w_scales[e][a][:, start:stop], w_grouped[e][a][:, start:stop, :])
 
         def multiply(c, e, a):
             features = slice(c * P, (c + 1) * P)
@@ -94,110 +114,106 @@ def tile_routed_moe_kernel(tc, xT, w, b, gate, offs, out):
                 rhs=x_codes[a][:, slots].bitcast(FP8X4),
                 rhs_scale=x_scales[a][:, slots],
                 start=(a == 0),
-                stop=(a == PASSES - 1),
+                stop=(a == LAST_PASS),
             )
 
         def activate(c, e):
-            nc.scalar.activation(ys[c][e][:], sums[c][e][:], GELU, bias=bias[:, c, e : e + 1])
+            nc.scalar.activation(activated[c][e][:], sums[c][e][:], GELU, bias=bias[:, e, c : c + 1])
 
         def scatter(c, e):
-            nc.vector.tensor_tensor(
-                windows[c][:].indirect(offsets[:, e * 16 : (e + 1) * 16]), ys[c][e][:], gates[:, e * C : (e + 1) * C], MULT
-            )
+            slots = slice(e * C, (e + 1) * C)
+            columns = slice(e * C // LIST_ROWS, (e + 1) * C // LIST_ROWS)
+            nc.vector.tensor_tensor(windows[c][:].indirect(offsets[:, columns]), activated[c][e][:], gates[:, slots], MULT)
 
         def store(c):
             nc.sync.dma_start(out[c * P : (c + 1) * P, :], windows[c][:])
 
+        nc.gpsimd.memset(bias_rows[:], 0.0)
+        make_identity(nc, identity[:])
         nc.sync.dma_start(offsets[:], offs)
-        load_x(0, 0)
-        load_x(0, 1)
-        load_x(0, 2)
-        load_x(0, 3)
-        load_x(1, 0)
-        load_x(1, 1)
-        load_x(1, 2)
-        load_x(1, 3)
-        load_x(2, 0)
-        load_x(2, 1)
-        load_x(2, 2)
-        load_x(2, 3)
-        load_w(0, 0)
-        load_w(0, 1)
-        load_w(0, 2)
-        nc.sync.dma_start(bias[:], b.rearrange("(c p) e -> p c e", p=P))
-        load_w(1, 0)
+        for a in range(PASSES):
+            for t in range(PACK):
+                load_x(a, t)
+            if a == 0:
+                nc.sync.dma_start(bias_rows[0:FEATURE_TILES, :], b.rearrange("(c p) e -> c (p e)", p=P))
+        for a in range(PASSES):
+            load_w(0, a)
         nc.sync.dma_start(gates[:], gate[0:P, :])
-        load_w(1, 1)
-        load_w(1, 2)
-        nc.vector.memset(warm[:], 0.0)
-        nc.scalar.activation(warmed[:], warm[:], GELU)
-        for c in range(BLOCKS):
+        for a in range(PASSES):
+            load_w(1, a)
+
+        nc.vector.memset(table_in[:], 0.0)
+        nc.scalar.activation(table_out[:], table_in[:], GELU)
+        for c in range(FEATURE_TILES):
             nc.gpsimd.memset(windows[c][:], 0.0)
+        for e in range(E):
+            nc.tensor.transpose(bias_columns[:, e, :], bias_rows[:, e::E], identity[:])
+        nc.vector.tensor_copy(bias[:], bias_columns[:, :, 0:FEATURE_TILES])
+
         for t in range(PACK):
             gather(0, t)
-        group_x(scopy, 0, 0, 512)
-        gather(1, 0)
-        gather(1, 1)
-        quant_x(0, 0, 512)
-        gather(1, 2)
-        gather(1, 3)
-        group_x(scopy, 1, 0, 512)
-        gather(2, 0)
-        gather(2, 1)
-        quant_x(1, 0, 512)
-        gather(2, 2)
-        gather(2, 3, 0, C)
-        group_x(vcopy, 2, 0, 128)
-        group_x(scopy, 2, 128, 256)
-        gather(2, 3, C, SLOTS)
-        group_w(scopy, 0, 0, 0, 256)
-        quant_x(2, 0, 256)
-        group_x(vcopy, 2, 256, 448)
-        group_w(scopy, 0, 0, 256, 384)
-        quant_w(0, 0, 0, 256)
-        group_w(vcopy, 0, 1, 0, 128)
-        group_w(scopy, 0, 1, 128, 256)
-        quant_w(0, 0, 256, 384)
-        group_w(scopy, 0, 1, 256, 384)
-        quant_w(0, 1, 0, 256)
-        group_w(vcopy, 0, 2, 0, 256)
+        for a in range(LAST_PASS):
+            group_x(by_scalar, a, 0, SLOTS)
+            gather(a + 1, 0)
+            gather(a + 1, 1)
+            quantize_x(a, 0, SLOTS)
+            for t in range(2, PACK):
+                if (a + 1, t) != (LAST_PASS, LAST_T):
+                    gather(a + 1, t)
+
+        gather(LAST_PASS, LAST_T, 0, C)
+        group_x(by_vector, LAST_PASS, 0, X_CUT[0])
+        group_x(by_scalar, LAST_PASS, X_CUT[0], C)
+        gather(LAST_PASS, LAST_T, C, SLOTS)
+        group_w(by_scalar, 0, 0, *TWO_TILES)
+        quantize_x(LAST_PASS, 0, C)
+        group_x(by_vector, LAST_PASS, C, X_CUT[1])
+        group_w(by_scalar, 0, 0, *ONE_TILE)
+        quantize_w(0, 0, TWO_TILES)
+        group_w(by_vector, 0, 1, 0, P)
+        group_w(by_scalar, 0, 1, P, 2 * P)
+        quantize_w(0, 0, ONE_TILE)
+        group_w(by_scalar, 0, 1, *ONE_TILE)
+        quantize_w(0, 1, TWO_TILES)
+        group_w(by_vector, 0, 2, *TWO_TILES)
         for c in (0, 1):
             multiply(c, 0, 0)
             multiply(c, 0, 1)
-        group_w(scopy, 0, 2, 256, 384)
-        quant_w(0, 2, 0, 256)
-        group_x(scopy, 2, 448, 512)
-        quant_w(0, 2, 256, 384)
+        group_w(by_scalar, 0, 2, *ONE_TILE)
+        quantize_w(0, 2, TWO_TILES)
+        group_x(by_scalar, LAST_PASS, X_CUT[1], SLOTS)
+        quantize_w(0, 2, ONE_TILE)
         multiply(0, 0, 2)
         multiply(1, 0, 2)
         activate(0, 0)
-        quant_x(2, 256, 512)
-        group_w(scopy, 1, 0, 192, 384)
-        quant_w(0, 1, 256, 384)
+        quantize_x(LAST_PASS, C, SLOTS)
+
+        group_w(by_scalar, 1, 0, W1_CUT, N)
+        quantize_w(0, 1, ONE_TILE)
         scatter(0, 0)
         for a in range(PASSES):
             multiply(2, 0, a)
-        group_w(scopy, 1, 0, 0, 192)
+        group_w(by_scalar, 1, 0, 0, W1_CUT)
         activate(1, 0)
-        quant_w(1, 0, 0, 256)
-        group_w(scopy, 1, 1, 192, 384)
-        quant_w(1, 0, 256, 384)
-        multiply(0, 1, 0)
-        multiply(1, 1, 0)
-        multiply(2, 1, 0)
+        quantize_w(1, 0, TWO_TILES)
+        group_w(by_scalar, 1, 1, W1_CUT, N)
+        quantize_w(1, 0, ONE_TILE)
+        for c in range(FEATURE_TILES):
+            multiply(c, 1, 0)
         scatter(1, 0)
         activate(2, 0)
-        group_w(scopy, 1, 2, 256, 384)
-        group_w(scopy, 1, 2, 0, 256)
-        quant_w(1, 2, 256, 384)
-        quant_w(1, 1, 256, 384)
+        group_w(by_scalar, 1, 2, *ONE_TILE)
+        group_w(by_scalar, 1, 2, *TWO_TILES)
+        quantize_w(1, 2, ONE_TILE)
+        quantize_w(1, 1, ONE_TILE)
         scatter(2, 0)
-        group_w(scopy, 1, 1, 0, 192)
+        group_w(by_scalar, 1, 1, 0, W1_CUT)
+
         multiply(2, 1, 1)
         multiply(2, 1, 2)
         activate(2, 1)
-        quant_w(1, 2, 0, 256)
-        quant_w(1, 1, 0, 256)
+        quantize_w(1, 2, TWO_TILES)
+        quantize_w(1, 1, TWO_TILES)
         scatter(2, 1)
         store(2)
         for c in (1, 0):

from contextlib import ExitStack

import concourse.mybir as mybir
from concourse.masks import make_identity

K, T, E, C, N = 1536, 1536, 2, 256, 384
SLOTS = E * C
P = 128
PACK = 4
K_PASS = P * PACK
PASSES = K // K_PASS
FEATURE_TILES = N // P
LIST_ROWS = 16
LAST_PASS, LAST_T = PASSES - 1, PACK - 1

TWO_TILES, ONE_TILE = (0, 2 * P), (2 * P, N)
X_CUT = (128, C + 192)
W1_CUT = 192

FLOPS = 2 * K * N * SLOTS

F32 = mybir.dt.float32
BF16 = mybir.dt.bfloat16
U32 = mybir.dt.uint32
U16 = mybir.dt.uint16
U8 = mybir.dt.uint8
FP8X4 = mybir.dt.float8_e4m3fn_x4
GELU = mybir.ActivationFunctionType.Gelu_apprx_tanh
MULT = mybir.AluOpType.mult


def interleave(copy, grouped, planes):
    copy(
        out=grouped.rearrange("p (n i) t -> p n t i", i=4),
        in_=planes.rearrange("p t (n i) -> p n t i", i=4),
    )


def quantize(nc, codes, scales, grouped):
    nc.vector.quantize_mx(
        out=codes.bitcast(FP8X4),
        scales=scales,
        in_=grouped.rearrange("p n t -> p (n t)"),
    )


def tile_routed_moe_kernel(tc, xT, w, b, gate, offs, out):
    nc = tc.nc
    by_scalar, by_vector = nc.scalar.copy, nc.vector.tensor_copy

    with ExitStack() as ctx:
        keep = ctx.enter_context(tc.tile_pool(name="keep", bufs=1))
        psum = ctx.enter_context(tc.psum_pool(name="psum", bufs=1))

        offsets = keep.tile([P, SLOTS // LIST_ROWS], U16, name="offsets")
        gates = keep.tile([P, SLOTS], F32, name="gates")
        bias = keep.tile([P, E, FEATURE_TILES], F32, name="bias")
        bias_rows = keep.tile([P, E * P], F32, name="bias_rows")
        identity = keep.tile([P, P], F32, name="identity")
        table_in = keep.tile([P, 1], F32, name="table_in")
        table_out = keep.tile([P, 1], F32, name="table_out")

        x_planes = [[keep.tile([P, T], F32, name=f"x_plane{a}{t}") for t in range(PACK)] for a in range(PASSES)]
        picked = [keep.tile([P, PACK, SLOTS], F32, name=f"picked{a}") for a in range(PASSES)]
        x_grouped = [keep.tile([P, SLOTS, PACK], BF16, name=f"x_grouped{a}", align_bytes=64) for a in range(PASSES)]
        x_codes = [keep.tile([P, SLOTS], U32, name=f"x_codes{a}", align_bytes=64) for a in range(PASSES)]
        x_scales = [keep.tile([P, SLOTS], U8, name=f"x_scales{a}", align_bytes=64) for a in range(PASSES)]

        def weight_tiles(name, shape, dtype):
            return [[keep.tile(shape, dtype, name=f"{name}{e}{a}", align_bytes=64) for a in range(PASSES)] for e in range(E)]

        w_raw = weight_tiles("w_raw", [P, PACK, N], F32)
        w_grouped = weight_tiles("w_grouped", [P, N, PACK], BF16)
        w_codes = weight_tiles("w_codes", [P, N], U32)
        w_scales = weight_tiles("w_scales", [P, N], U8)

        windows = [keep.tile([P, T], F32, name=f"window{c}") for c in range(FEATURE_TILES)]
        activated = [[keep.tile([P, C], F32, name=f"activated{c}{e}") for e in range(E)] for c in range(FEATURE_TILES)]
        sums = [[psum.tile([P, C], F32, name=f"sums{c}{e}") for e in range(E)] for c in range(FEATURE_TILES)]
        bias_columns = psum.tile([P, E, P], F32, name="bias_columns")

        def load_x(a, t):
            rows = xT.rearrange("(a p t) n -> a p t n", p=P, t=PACK)
            nc.sync.dma_start(x_planes[a][t][:], rows[a, :, t, :])

        def load_w(e, a):
            rows = w[e, a * K_PASS : (a + 1) * K_PASS, :]
            nc.sync.dma_start(w_raw[e][a][:], rows.rearrange("(p t) n -> p t n", t=PACK))

        def gather(a, t, start=0, stop=SLOTS):
            columns = slice(start // LIST_ROWS, stop // LIST_ROWS)
            nc.vector.tensor_copy(picked[a][:, t, start:stop], x_planes[a][t][:].indirect(offsets[:, columns]))

        def group_x(copy, a, start, stop):
            interleave(copy, x_grouped[a][:, start:stop, :], picked[a][:, :, start:stop])

        def quantize_x(a, start, stop):
            quantize(nc, x_codes[a][:, start:stop], x_scales[a][:, start:stop], x_grouped[a][:, start:stop, :])

        def group_w(copy, e, a, start, stop):
            interleave(copy, w_grouped[e][a][:, start:stop, :], w_raw[e][a][:, :, start:stop])

        def quantize_w(e, a, features):
            start, stop = features
            quantize(nc, w_codes[e][a][:, start:stop], w_scales[e][a][:, start:stop], w_grouped[e][a][:, start:stop, :])

        def multiply(c, e, a):
            features = slice(c * P, (c + 1) * P)
            slots = slice(e * C, (e + 1) * C)
            nc.tensor.matmul_mx(
                out=sums[c][e][:],
                lhsT=w_codes[e][a][:, features].bitcast(FP8X4),
                lhsT_scale=w_scales[e][a][:, features],
                rhs=x_codes[a][:, slots].bitcast(FP8X4),
                rhs_scale=x_scales[a][:, slots],
                start=(a == 0),
                stop=(a == LAST_PASS),
            )

        def activate(c, e):
            nc.scalar.activation(activated[c][e][:], sums[c][e][:], GELU, bias=bias[:, e, c : c + 1])

        def scatter(c, e):
            slots = slice(e * C, (e + 1) * C)
            columns = slice(e * C // LIST_ROWS, (e + 1) * C // LIST_ROWS)
            nc.vector.tensor_tensor(windows[c][:].indirect(offsets[:, columns]), activated[c][e][:], gates[:, slots], MULT)

        def store(c):
            nc.sync.dma_start(out[c * P : (c + 1) * P, :], windows[c][:])

        nc.gpsimd.memset(bias_rows[:], 0.0)
        make_identity(nc, identity[:])
        nc.sync.dma_start(offsets[:], offs)
        for a in range(PASSES):
            for t in range(PACK):
                load_x(a, t)
            if a == 0:
                nc.sync.dma_start(bias_rows[0:FEATURE_TILES, :], b.rearrange("(c p) e -> c (p e)", p=P))
        for a in range(PASSES):
            load_w(0, a)
        nc.sync.dma_start(gates[:], gate[0:P, :])
        for a in range(PASSES):
            load_w(1, a)

        nc.vector.memset(table_in[:], 0.0)
        nc.scalar.activation(table_out[:], table_in[:], GELU)
        for c in range(FEATURE_TILES):
            nc.gpsimd.memset(windows[c][:], 0.0)
        for e in range(E):
            nc.tensor.transpose(bias_columns[:, e, :], bias_rows[:, e::E], identity[:])
        nc.vector.tensor_copy(bias[:], bias_columns[:, :, 0:FEATURE_TILES])

        for t in range(PACK):
            gather(0, t)
        for a in range(LAST_PASS):
            group_x(by_scalar, a, 0, SLOTS)
            gather(a + 1, 0)
            gather(a + 1, 1)
            quantize_x(a, 0, SLOTS)
            for t in range(2, PACK):
                if (a + 1, t) != (LAST_PASS, LAST_T):
                    gather(a + 1, t)

        gather(LAST_PASS, LAST_T, 0, C)
        group_x(by_vector, LAST_PASS, 0, X_CUT[0])
        group_x(by_scalar, LAST_PASS, X_CUT[0], C)
        gather(LAST_PASS, LAST_T, C, SLOTS)
        group_w(by_scalar, 0, 0, *TWO_TILES)
        quantize_x(LAST_PASS, 0, C)
        group_x(by_vector, LAST_PASS, C, X_CUT[1])
        group_w(by_scalar, 0, 0, *ONE_TILE)
        quantize_w(0, 0, TWO_TILES)
        group_w(by_vector, 0, 1, 0, P)
        group_w(by_scalar, 0, 1, P, 2 * P)
        quantize_w(0, 0, ONE_TILE)
        group_w(by_scalar, 0, 1, *ONE_TILE)
        quantize_w(0, 1, TWO_TILES)
        group_w(by_vector, 0, 2, *TWO_TILES)
        for c in (0, 1):
            multiply(c, 0, 0)
            multiply(c, 0, 1)
        group_w(by_scalar, 0, 2, *ONE_TILE)
        quantize_w(0, 2, TWO_TILES)
        group_x(by_scalar, LAST_PASS, X_CUT[1], SLOTS)
        quantize_w(0, 2, ONE_TILE)
        multiply(0, 0, 2)
        multiply(1, 0, 2)
        activate(0, 0)
        quantize_x(LAST_PASS, C, SLOTS)

        group_w(by_scalar, 1, 0, W1_CUT, N)
        quantize_w(0, 1, ONE_TILE)
        scatter(0, 0)
        for a in range(PASSES):
            multiply(2, 0, a)
        group_w(by_scalar, 1, 0, 0, W1_CUT)
        activate(1, 0)
        quantize_w(1, 0, TWO_TILES)
        group_w(by_scalar, 1, 1, W1_CUT, N)
        quantize_w(1, 0, ONE_TILE)
        for c in range(FEATURE_TILES):
            multiply(c, 1, 0)
        scatter(1, 0)
        activate(2, 0)
        group_w(by_scalar, 1, 2, *ONE_TILE)
        group_w(by_scalar, 1, 2, *TWO_TILES)
        quantize_w(1, 2, ONE_TILE)
        quantize_w(1, 1, ONE_TILE)
        scatter(2, 0)
        group_w(by_scalar, 1, 1, 0, W1_CUT)

        multiply(2, 1, 1)
        multiply(2, 1, 2)
        activate(2, 1)
        quantize_w(1, 2, TWO_TILES)
        quantize_w(1, 1, TWO_TILES)
        scatter(2, 1)
        store(2)
        for c in (1, 0):
            multiply(c, 1, 1)
            multiply(c, 1, 2)
            activate(c, 1)
        for c in (1, 0):
            scatter(c, 1)
            store(c)
